import numpy as np
import ml_dtypes


def mxq(x, axis, fmt="e4m3"):
    dtype, down = {"e4m3": (ml_dtypes.float8_e4m3fn, 7), "e5m2": (ml_dtypes.float8_e5m2, 14)}[fmt]
    v = np.moveaxis(np.asarray(x, np.float32).astype(ml_dtypes.bfloat16).astype(np.float64), axis, -1)
    blocks = v.reshape(v.shape[:-1] + (-1, 32))
    amax = np.abs(blocks).max(-1, keepdims=True)
    byte = np.maximum(np.where(amax > 0, np.frexp(amax)[1] - 1 + 127, 0) - down, 1)
    scale = np.exp2(byte - 127.0)
    codes = (blocks / scale).astype(np.float32).astype(dtype).astype(np.float64)
    return np.moveaxis((codes * scale).reshape(v.shape), -1, axis)


WIDE = False


def mx_kscale(k):
    if not WIDE:
        return np.ones(k)
    levels = np.array([30, -30])
    if k % 512:
        return np.exp2(np.random.permutation(np.resize(levels, k // 32))).repeat(32)
    a = np.empty((k // 512, 16))
    for p in range(k // 512):
        a[p, :8] = np.random.permutation(np.resize(levels, 8))
        for g in range(8):
            far = levels[np.abs(levels - a[p, g]) >= 10]
            a[p, g + 8] = far[np.random.randint(len(far))]
    return np.exp2(a.ravel()).repeat(32)


def f64(x):
    return np.asarray(x).astype(np.float64)


def striped(idx):
    return np.tile(np.asarray(idx).reshape(-1, 16).T, (8, 1)).astype(np.uint16)


def unstriped(offs):
    return offs[:16].T.reshape(-1).astype(np.int64)


E2M1 = np.array([0.0, 0.5, 1.0, 1.5, 2.0, 3.0, 4.0, 6.0, -0.0, -0.5, -1.0, -1.5, -2.0, -3.0, -4.0, -6.0])


def pack_weight(w, fmt):
    k, n = w.shape
    w = f64(np.asarray(w, np.float32).astype(ml_dtypes.bfloat16)).reshape(k // 32, 32, n)
    amax = np.abs(w).max(1)
    if fmt in ("e4m3", "e5m2"):
        byte = np.frexp(amax)[1] - 1 + 127 - (7 if fmt == "e4m3" else 14)
    else:
        mant, ex = np.frexp(amax / 6.0)
        byte = np.where(mant > 0.5, ex, ex - 1) + 127
    byte = np.clip(np.where(amax > 0, byte, 1), 1, 254)
    scaled = (w * np.exp2(127.0 - byte)[:, None, :]).reshape(k, n).astype(np.float32)
    by_word = np.ascontiguousarray(scaled.reshape(k // 512, 128, 4, n).transpose(0, 1, 3, 2))
    if fmt in ("e4m3", "e5m2"):
        words = by_word.astype(ml_dtypes.float8_e4m3fn if fmt == "e4m3" else ml_dtypes.float8_e5m2).view(np.uint8)
    else:
        c = by_word.astype(ml_dtypes.float4_e2m1fn).view(np.uint8) & 0xF
        words = (c[..., 0::2] | (c[..., 1::2] << 4)).reshape(k // 512, 128, 2 * n)
    return np.ascontiguousarray(words), np.ascontiguousarray(byte.astype(np.uint8).reshape(k // 512, 16, n))


def unpack_weight(words, scales, fmt):
    g, _, n = scales.shape
    words = np.ascontiguousarray(words).reshape(g, 128, n, -1)
    if fmt in ("e4m3", "e5m2"):
        vals = words.view(ml_dtypes.float8_e4m3fn if fmt == "e4m3" else ml_dtypes.float8_e5m2).astype(np.float64)
    else:
        nib = np.empty((g, 128, n, 4), np.uint8)
        nib[..., 0::2] = words & 0xF
        nib[..., 1::2] = words >> 4
        vals = E2M1[nib]
    vals = vals * np.repeat(np.exp2(scales.astype(np.float64) - 127.0), 8, axis=1)[..., None]
    return vals.transpose(0, 1, 3, 2).reshape(g * 512, n)


def bf(x):
    return np.asarray(x, np.float32).astype(ml_dtypes.bfloat16)


def planes(Y):
    r, m = Y.shape
    b = f64(bf(Y)).reshape(r // 32, 32, m)
    amax = np.abs(b).max(1)
    byte = np.clip(np.where(amax > 0, np.frexp(amax)[1] - 1 + 127 - 7, 1), 1, 254)
    codes = (b * np.exp2(127.0 - byte)[:, None, :]).reshape(r, m).astype(np.float32).astype(ml_dtypes.float8_e4m3fn).view(np.uint8)
    words = codes.reshape(r // 512, 128, 4, m).transpose(0, 1, 3, 2)
    return np.ascontiguousarray(words), np.ascontiguousarray(byte.astype(np.uint8).reshape(r // 512, 16, m))


K, T, J, S, R, C, O, N = 1024, 1024, 256, 512, 512, 1024, 256, 512


def setup_inputs():
    n = np.random.standard_normal
    idx = np.random.permutation(T)[:J]
    idx2 = np.random.permutation(S)[:J]
    idx3 = np.random.permutation(C)[:J]
    idx4 = np.random.permutation(C)[:O]
    fk = mx_kscale(K)
    fr = mx_kscale(R)
    wp = pack_weight(n((K, R)) * 1 / np.sqrt(K) * fk[:, None] * fr, "e5m2")
    wbp = pack_weight(n((R, N)) * 1 / np.sqrt(R) / fr[:, None], "e2m1")
    return {
        "xa": (n((K, T))).astype(np.float32),
        "xb": (n((K, S))).astype(np.float32),
        "fk": (np.random.uniform(0.5, 2.0, (K, 1)) / fk[:, None]).astype(np.float32),
        "w_words": wp[0],
        "w_scales": wp[1],
        "oldh": (n((R, C)) * 0.7 * fr[:, None]).astype(np.float32),
        "wb_words": wbp[0],
        "wb_scales": wbp[1],
        "rs": (n((N, O))).astype(np.float32),
        "offs": striped(idx),
        "offs2": striped(idx2),
        "offs3": striped(idx3),
        "offs4": striped(idx4),
    }


def reference(xa, xb, fk, w_words, w_scales, oldh, wb_words, wb_scales, rs, offs, offs2, offs3, offs4):
    idx = unstriped(offs)
    idx2 = unstriped(offs2)
    idx3 = unstriped(offs3)
    idx4 = unstriped(offs4)
    wu = unpack_weight(w_words, w_scales, "e5m2")
    wbu = unpack_weight(wb_words, wb_scales, "e2m1")
    u = f64(xa)[:, idx] * f64(xb)[:, idx2] * f64(fk)
    uq = mxq(u, 0, "e5m2")
    a = wu.T @ uq
    ha = np.maximum(a, 0.0)
    pw0 = np.zeros((R, C))
    pw0[:, idx3] = ha
    pg = pw0 + f64(oldh)
    hid = pg[:, idx4]
    hidq = mxq(hid, 0, "e5m2")
    p = wbu.T @ hidq
    p1 = np.pad(p, ((0, 0), (1, 0)))[:, :O]
    y = p - 0.7 * p1 + 0.5 * f64(rs)
    words, scales = planes(y)
    return y, words, scales

@@ -1,0 +1,212 @@
+from contextlib import ExitStack
+
+import concourse.mybir as mybir
+
+K, T, J, S, R, C, O, N = 1024, 1024, 256, 512, 512, 1024, 256, 512
+FLOPS = 2 * K * R * J + 2 * R * N * O
+
+F32 = mybir.dt.float32
+BF16 = mybir.dt.bfloat16
+I32 = mybir.dt.int32
+U32 = mybir.dt.uint32
+U16 = mybir.dt.uint16
+U8 = mybir.dt.uint8
+E5M2 = mybir.dt.float8_e5m2_x4
+E4M3 = mybir.dt.float8_e4m3fn_x4
+E2M1 = mybir.dt.float4_e2m1fn_x4
+MULT = mybir.AluOpType.mult
+ADD = mybir.AluOpType.add
+COPY = mybir.ActivationFunctionType.Copy
+RELU = mybir.ActivationFunctionType.Relu
+
+P = 128
+PACK = 4
+PASSES = K // (P * PACK)
+
+
+def interleave(nc, dst, src):
+    nc.vector.tensor_copy(
+        out=dst.rearrange("p (c i) t -> p c t i", i=4),
+        in_=src.rearrange("p t (c i) -> p c t i", i=4),
+    )
+
+
+def tile_list_page_entryproducts_lagged_pl_kernel(
+    tc, xa, xb, fk, w_words, w_scales, oldh, wb_words, wb_scales, rs,
+    offs, offs2, offs3, offs4, out_0, out_1, out_2,
+):
+    nc = tc.nc
+    with ExitStack() as ctx:
+        lists = ctx.enter_context(tc.tile_pool(name="lists", bufs=1))
+        sb = ctx.enter_context(tc.tile_pool(name="sb", bufs=1))
+        psum = ctx.enter_context(tc.psum_pool(name="psum", bufs=1))
+
+        o1 = lists.tile([P, J // 16], U16, name="o1")
+        o2 = lists.tile([P, J // 16], U16, name="o2")
+        o3 = lists.tile([P, J // 16], U16, name="o3")
+        o4 = lists.tile([P, O // 16], U16, name="o4")
+
+        xa_v = xa.rearrange("(z p t) c -> z p t c", p=P, t=PACK)
+        xb_v = xb.rearrange("(z p t) c -> z p t c", p=P, t=PACK)
+        old_v = oldh.rearrange("(p t) c -> p t c", t=PACK)
+
+        xa_sb = [[sb.tile([P, T], F32, name=f"xa{z}{t}") for t in range(PACK)] for z in range(PASSES)]
+        xb_sb = [sb.tile([P, PACK, S], F32, name=f"xb{z}") for z in range(PASSES)]
+        fk_sb = sb.tile([P, PASSES, PACK], F32, name="fk_sb")
+        w_raw = [sb.tile([P, R], U32, name=f"w_raw{z}") for z in range(PASSES)]
+        ws_raw = sb.tile([P, PASSES, R], U8, name="ws_raw")
+        wb_raw = sb.tile([P, 2 * N], U8, name="wb_raw")
+        wbs_raw = sb.tile([P, N], U8, name="wbs_raw")
+        old_sb = [sb.tile([P, C], F32, name=f"old{t}") for t in range(PACK)]
+        rs_sb = sb.tile([P, PACK, O], F32, name="rs_sb")
+        placed = [sb.tile([P, C], F32, name=f"placed{t}") for t in range(PACK)]
+        page = [sb.tile([P, C], F32, name=f"page{t}") for t in range(PACK)]
+
+        nc.vector.memset(ws_raw[:].bitcast(I32), 0)
+        nc.vector.memset(wbs_raw[:].bitcast(I32), 0)
+        for t in range(PACK):
+            nc.vector.memset(placed[t][:], 0.0)
+
+        def load_w(z):
+            nc.sync.dma_start(
+                out=w_raw[z][:].bitcast(I32),
+                in_=w_words[z].rearrange("p c t -> p (c t)").bitcast(I32),
+            )
+
+        def load_xa(z, t):
+            nc.sync.dma_start(out=xa_sb[z][t][:], in_=xa_v[z, :, t, :])
+
+        def load_ws(q):
+            nc.sync.dma_start(
+                out=ws_raw[32 * q : 32 * q + 4, :, :].bitcast(I32),
+                in_=w_scales[:, 4 * q : 4 * q + 4, :].rearrange("z r c -> r z c").bitcast(I32),
+            )
+
+        def load_wbs(q):
+            nc.sync.dma_start(
+                out=wbs_raw[32 * q : 32 * q + 4, :].bitcast(I32),
+                in_=wb_scales[0, 4 * q : 4 * q + 4, :].bitcast(I32),
+            )
+
+        nc.sync.dma_start(out=xb_sb[0][:], in_=xb_v[0])
+        load_xa(0, 0)
+        nc.sync.dma_start(o2[:], offs2)
+        nc.sync.dma_start(o1[:], offs)
+        nc.sync.dma_start(out=fk_sb[:], in_=fk.rearrange("(z p t) o -> p z (t o)", p=P, t=PACK))
+        load_xa(0, 1)
+        load_ws(0)
+        load_ws(1)
+        load_xa(0, 2)
+        load_ws(2)
+        load_ws(3)
+        load_xa(0, 3)
+        load_w(0)
+        nc.sync.dma_start(out=xb_sb[1][:], in_=xb_v[1])
+        load_wbs(0)
+        load_wbs(1)
+        load_xa(1, 0)
+        load_wbs(2)
+        load_wbs(3)
+        load_xa(1, 1)
+        nc.sync.dma_start(o3[:], offs3)
+        nc.sync.dma_start(o4[:], offs4)
+        load_xa(1, 2)
+        load_xa(1, 3)
+        load_w(1)
+        nc.sync.dma_start(out=wb_raw[:].bitcast(I32), in_=wb_words[0].bitcast(I32))
+        for t in (0, 3, 1, 2):
+            nc.sync.dma_start(out=old_sb[t][:], in_=old_v[:, t, :])
+        nc.sync.dma_start(out=rs_sb[:], in_=rs.rearrange("(p t) o -> p t o", t=PACK))
+
+        w_sb = [sb.tile([P, PACK, P], U32, name=f"w_sb{z}", align_bytes=64) for z in range(PASSES)]
+        ws_sb = sb.tile([P, PASSES, PACK, P], U8, name="ws_sb", align_bytes=64)
+        wbs_sb = sb.tile([P, PACK, P], U8, name="wbs_sb", align_bytes=64)
+
+        acc = [psum.tile([P, J], F32, name=f"acc{t}") for t in range(PACK)]
+        for z in range(PASSES):
+            u32 = sb.tile([P, PACK, J], F32, name=f"u32_{z}")
+            for t in range(PACK):
+                picked = sb.tile([P, J], F32, name=f"picked{z}{t}")
+                scaled = sb.tile([P, J], F32, name=f"scaled{z}{t}")
+                nc.scalar.activation(picked[:], xb_sb[z][:, t, :].indirect(o2[:]), COPY)
+                nc.scalar.activation(scaled[:], picked[:], COPY, scale=fk_sb[:, z, t : t + 1])
+                nc.vector.tensor_tensor(u32[:, t, :], xa_sb[z][t][:].indirect(o1[:]), scaled[:], MULT)
+            u16 = sb.tile([P, J, PACK], BF16, name=f"u16_{z}", tag=f"u16_{z}", align_bytes=64)
+            interleave(nc, u16[:], u32[:])
+            nc.vector.tensor_copy(
+                out=w_sb[z][:].bitcast(I32),
+                in_=w_raw[z][:].bitcast(I32).rearrange("p (q t) -> p t q", t=PACK),
+            )
+            if z == 0:
+                nc.vector.tensor_copy(out=ws_sb[:], in_=ws_raw[:].rearrange("p z (q t) -> p z t q", t=PACK))
+                nc.vector.tensor_copy(out=wbs_sb[:], in_=wbs_raw[:].rearrange("p (q t) -> p t q", t=PACK))
+            u_codes = sb.tile([P, J], U32, name=f"u_codes{z}", align_bytes=64)
+            u_scales = sb.tile([P, J], U8, name=f"u_scales{z}", align_bytes=64)
+            nc.vector.quantize_mx(
+                out=u_codes[:].bitcast(E5M2), scales=u_scales[:], in_=u16[:].rearrange("p c t -> p (c t)")
+            )
+            for t in range(PACK):
+                nc.tensor.matmul_mx(
+                    out=acc[t][:],
+                    lhsT=w_sb[z][:, t, :].bitcast(E5M2),
+                    lhsT_scale=ws_sb[:, z, t, :],
+                    rhs=u_codes[:].bitcast(E5M2),
+                    rhs_scale=u_scales[:],
+                    start=(z == 0),
+                    stop=(z == PASSES - 1),
+                )
+
+        wb_sb = sb.tile([P, PACK, P, 2], U8, name="wb_sb", tag="u16_1", align_bytes=64)
+        nc.vector.tensor_copy(out=wb_sb[:], in_=wb_raw[:].rearrange("p (q t b) -> p t q b", t=PACK, b=2))
+        ha = [sb.tile([P, J], F32, name=f"ha{t}") for t in range(PACK)]
+        nc.scalar.activation(ha[0][:], acc[0][:], RELU)
+        for t in range(1, PACK):
+            nc.vector.tensor_scalar_max(ha[t][:], acc[t][:], 0.0)
+        for t in range(PACK - 1):
+            nc.scalar.activation(placed[t][:].indirect(o3[:]), ha[t][:], COPY)
+        nc.vector.tensor_copy(placed[3][:].indirect(o3[:]), ha[3][:])
+        hid = sb.tile([P, PACK, O], BF16, name="hid")
+        for t in (0, 3, 1, 2):
+            nc.vector.tensor_tensor(page[t][:], placed[t][:], old_sb[t][:], ADD)
+            nc.scalar.activation(hid[:, t, :], page[t][:].indirect(o4[:]), COPY)
+        hid16 = sb.tile([P, O, PACK], BF16, name="hid16", align_bytes=64)
+        interleave(nc, hid16[:], hid[:])
+        h_codes = sb.tile([P, O], U32, name="h_codes", align_bytes=64)
+        h_scales = sb.tile([P, O], U8, name="h_scales", align_bytes=64)
+        nc.vector.quantize_mx(
+            out=h_codes[:].bitcast(E5M2), scales=h_scales[:], in_=hid16[:].rearrange("p c t -> p (c t)")
+        )
+        y = sb.tile([P, PACK, O], F32, name="y")
+        for b in range(2):
+            bank = psum.tile([P, 2, O], F32, name=f"bank{b}")
+            for s in range(2):
+                t = 2 * b + s
+                nc.tensor.matmul_mx(
+                    out=bank[:, s, :],
+                    lhsT=wb_sb[:, t, :, :].rearrange("p q b -> p (q b)").bitcast(E2M1),
+                    lhsT_scale=wbs_sb[:, t, :],
+                    rhs=h_codes[:].bitcast(E5M2),
+                    rhs_scale=h_scales[:],
+                    start=True,
+                    stop=True,
+                )
+            rows = slice(2 * b, 2 * b + 2)
+            nc.vector.scalar_tensor_tensor(y[:, rows, :], rs_sb[:, rows, :], 0.5, bank[:], MULT, ADD)
+            nc.vector.scalar_tensor_tensor(
+                y[:, rows, 1:O], bank[:, :, 0 : O - 1], -0.7, y[:, rows, 1:O], MULT, ADD
+            )
+        nc.sync.dma_start(out=out_0.rearrange("(p t) o -> p t o", t=PACK), in_=y[:])
+        y16 = sb.tile([P, O, PACK], BF16, name="y16", align_bytes=64)
+        interleave(nc, y16[:], y[:])
+        y_codes = sb.tile([P, O], U32, name="y_codes", align_bytes=64)
+        y_scales = sb.tile([P, O], U8, name="y_scales", align_bytes=64)
+        nc.vector.quantize_mx(
+            out=y_codes[:].bitcast(E4M3), scales=y_scales[:], in_=y16[:].rearrange("p c t -> p (c t)")
+        )
+        nc.sync.dma_start(out=out_1[0].rearrange("p c t -> p (c t)").bitcast(I32), in_=y_codes[:].bitcast(I32))
+        for q in range(4):
+            eng = nc.scalar if q >= 1 else nc.sync
+            eng.dma_start(
+                out=out_2[0, 4 * q : 4 * q + 4, :].bitcast(I32),
+                in_=y_scales[32 * q : 32 * q + 4, :].bitcast(I32),
+            )

@@ -24,8 +24,8 @@ PACK = 4
 PASSES = K // (P * PACK)
 
 
-def interleave(nc, dst, src):
-    nc.vector.tensor_copy(
+def interleave(copy, dst, src):
+    copy(
         out=dst.rearrange("p (c i) t -> p c t i", i=4),
         in_=src.rearrange("p t (c i) -> p c t i", i=4),
     )
@@ -51,13 +51,13 @@ def tile_list_page_entryproducts_lagged_pl_kernel(
         old_v = oldh.rearrange("(p t) c -> p t c", t=PACK)
 
         xa_sb = [[sb.tile([P, T], F32, name=f"xa{z}{t}") for t in range(PACK)] for z in range(PASSES)]
-        xb_sb = [sb.tile([P, PACK, S], F32, name=f"xb{z}") for z in range(PASSES)]
+        xb_sb = [[sb.tile([P, 2, S], F32, name=f"xb{z}{h}") for h in range(2)] for z in range(PASSES)]
         fk_sb = sb.tile([P, PASSES, PACK], F32, name="fk_sb")
         w_raw = [sb.tile([P, R], U32, name=f"w_raw{z}") for z in range(PASSES)]
         ws_raw = sb.tile([P, PASSES, R], U8, name="ws_raw")
         wb_raw = sb.tile([P, 2 * N], U8, name="wb_raw")
         wbs_raw = sb.tile([P, N], U8, name="wbs_raw")
-        old_sb = [sb.tile([P, C], F32, name=f"old{t}") for t in range(PACK)]
+        old_sb = [sb.tile([P, C], F32, name=f"old{t}", tag=f"old{t}", align_bytes=64) for t in range(PACK)]
         rs_sb = sb.tile([P, PACK, O], F32, name="rs_sb")
         placed = [sb.tile([P, C], F32, name=f"placed{t}") for t in range(PACK)]
         page = [sb.tile([P, C], F32, name=f"page{t}") for t in range(PACK)]
@@ -88,58 +88,58 @@ def tile_list_page_entryproducts_lagged_pl_kernel(
                 in_=wb_scales[0, 4 * q : 4 * q + 4, :].bitcast(I32),
             )
 
-        nc.sync.dma_start(out=xb_sb[0][:], in_=xb_v[0])
+        def load_xb(z, h):
+            nc.sync.dma_start(out=xb_sb[z][h][:], in_=xb_v[z, :, 2 * h : 2 * h + 2, :])
+
+        load_xb(0, 0)
         load_xa(0, 0)
         nc.sync.dma_start(o2[:], offs2)
         nc.sync.dma_start(o1[:], offs)
         nc.sync.dma_start(out=fk_sb[:], in_=fk.rearrange("(z p t) o -> p z (t o)", p=P, t=PACK))
+        load_xb(0, 1)
         load_xa(0, 1)
         load_ws(0)
         load_ws(1)
         load_xa(0, 2)
         load_ws(2)
         load_ws(3)
+        load_xb(1, 0)
         load_xa(0, 3)
         load_w(0)
-        nc.sync.dma_start(out=xb_sb[1][:], in_=xb_v[1])
-        load_wbs(0)
-        load_wbs(1)
         load_xa(1, 0)
-        load_wbs(2)
-        load_wbs(3)
-        load_xa(1, 1)
         nc.sync.dma_start(o3[:], offs3)
         nc.sync.dma_start(o4[:], offs4)
-        load_xa(1, 2)
-        load_xa(1, 3)
+        load_xb(1, 1)
+        for t in range(1, PACK):
+            load_xa(1, t)
         load_w(1)
         nc.sync.dma_start(out=wb_raw[:].bitcast(I32), in_=wb_words[0].bitcast(I32))
-        for t in (0, 3, 1, 2):
+        for t in range(PACK):
             nc.sync.dma_start(out=old_sb[t][:], in_=old_v[:, t, :])
+            load_wbs(t)
         nc.sync.dma_start(out=rs_sb[:], in_=rs.rearrange("(p t) o -> p t o", t=PACK))
 
         w_sb = [sb.tile([P, PACK, P], U32, name=f"w_sb{z}", align_bytes=64) for z in range(PASSES)]
         ws_sb = sb.tile([P, PASSES, PACK, P], U8, name="ws_sb", align_bytes=64)
-        wbs_sb = sb.tile([P, PACK, P], U8, name="wbs_sb", align_bytes=64)
 
         acc = [psum.tile([P, J], F32, name=f"acc{t}") for t in range(PACK)]
         for z in range(PASSES):
-            u32 = sb.tile([P, PACK, J], F32, name=f"u32_{z}")
+            u32 = [sb.tile([P, 2, J], F32, name=f"u32_{z}{h}") for h in range(2)]
+            u16 = sb.tile([P, J, PACK], BF16, name=f"u16_{z}", tag=f"u16_{z}", align_bytes=64)
             for t in range(PACK):
                 picked = sb.tile([P, J], F32, name=f"picked{z}{t}")
                 scaled = sb.tile([P, J], F32, name=f"scaled{z}{t}")
-                nc.scalar.activation(picked[:], xb_sb[z][:, t, :].indirect(o2[:]), COPY)
+                nc.scalar.activation(picked[:], xb_sb[z][t // 2][:, t % 2, :].indirect(o2[:]), COPY)
                 nc.scalar.activation(scaled[:], picked[:], COPY, scale=fk_sb[:, z, t : t + 1])
-                nc.vector.tensor_tensor(u32[:, t, :], xa_sb[z][t][:].indirect(o1[:]), scaled[:], MULT)
-            u16 = sb.tile([P, J, PACK], BF16, name=f"u16_{z}", tag=f"u16_{z}", align_bytes=64)
-            interleave(nc, u16[:], u32[:])
+                nc.vector.tensor_tensor(u32[t // 2][:, t % 2, :], xa_sb[z][t][:].indirect(o1[:]), scaled[:], MULT)
+                if t % 2 == 1:
+                    interleave(nc.vector.tensor_copy, u16[:, :, t - 1 : t + 1], u32[t // 2][:])
             nc.vector.tensor_copy(
                 out=w_sb[z][:].bitcast(I32),
                 in_=w_raw[z][:].bitcast(I32).rearrange("p (q t) -> p t q", t=PACK),
             )
             if z == 0:
                 nc.vector.tensor_copy(out=ws_sb[:], in_=ws_raw[:].rearrange("p z (q t) -> p z t q", t=PACK))
-                nc.vector.tensor_copy(out=wbs_sb[:], in_=wbs_raw[:].rearrange("p (q t) -> p t q", t=PACK))
             u_codes = sb.tile([P, J], U32, name=f"u_codes{z}", align_bytes=64)
             u_scales = sb.tile([P, J], U8, name=f"u_scales{z}", align_bytes=64)
             nc.vector.quantize_mx(
@@ -156,56 +156,64 @@ def tile_list_page_entryproducts_lagged_pl_kernel(
                     stop=(z == PASSES - 1),
                 )
 
-        wb_sb = sb.tile([P, PACK, P, 2], U8, name="wb_sb", tag="u16_1", align_bytes=64)
-        nc.vector.tensor_copy(out=wb_sb[:], in_=wb_raw[:].rearrange("p (q t b) -> p t q b", t=PACK, b=2))
+        wb_sb = sb.tile([P, PACK, P], U16, name="wb_sb", tag="u16_1", align_bytes=64)
+        nc.vector.tensor_copy(out=wb_sb[:], in_=wb_raw[:].bitcast(U16).rearrange("p (q t) -> p t q", t=PACK))
         ha = [sb.tile([P, J], F32, name=f"ha{t}") for t in range(PACK)]
         nc.scalar.activation(ha[0][:], acc[0][:], RELU)
         for t in range(1, PACK):
             nc.vector.tensor_scalar_max(ha[t][:], acc[t][:], 0.0)
-        for t in range(PACK - 1):
+        for t in (0, 2, 3):
             nc.scalar.activation(placed[t][:].indirect(o3[:]), ha[t][:], COPY)
-        nc.vector.tensor_copy(placed[3][:].indirect(o3[:]), ha[3][:])
-        hid = sb.tile([P, PACK, O], BF16, name="hid")
-        for t in (0, 3, 1, 2):
+        nc.vector.tensor_copy(placed[1][:].indirect(o3[:]), ha[1][:])
+        H = O // 2
+        hid = [sb.tile([P, PACK, H], BF16, name=f"hid{h}") for h in range(2)]
+        for t in range(PACK):
             nc.vector.tensor_tensor(page[t][:], placed[t][:], old_sb[t][:], ADD)
-            nc.scalar.activation(hid[:, t, :], page[t][:].indirect(o4[:]), COPY)
-        hid16 = sb.tile([P, O, PACK], BF16, name="hid16", align_bytes=64)
-        interleave(nc, hid16[:], hid[:])
-        h_codes = sb.tile([P, O], U32, name="h_codes", align_bytes=64)
-        h_scales = sb.tile([P, O], U8, name="h_scales", align_bytes=64)
-        nc.vector.quantize_mx(
-            out=h_codes[:].bitcast(E5M2), scales=h_scales[:], in_=hid16[:].rearrange("p c t -> p (c t)")
-        )
-        y = sb.tile([P, PACK, O], F32, name="y")
-        for b in range(2):
-            bank = psum.tile([P, 2, O], F32, name=f"bank{b}")
-            for s in range(2):
-                t = 2 * b + s
+            for h in range(2):
+                nc.scalar.activation(hid[h][:, t, :], page[t][:].indirect(o4[:, 8 * h : 8 * h + 8]), COPY)
+        wbs_sb = sb.tile([P, PACK, P], U8, name="wbs_sb", tag="old3", align_bytes=64)
+        nc.vector.tensor_copy(out=wbs_sb[:], in_=wbs_raw[:].rearrange("p (q t) -> p t q", t=PACK))
+        hid16 = [sb.tile([P, H, PACK], BF16, name=f"hid16_{h}", align_bytes=64) for h in range(2)]
+        h_codes = [sb.tile([P, H], U32, name=f"h_codes{h}", align_bytes=64) for h in range(2)]
+        h_scales = [sb.tile([P, H], U8, name=f"h_scales{h}", align_bytes=64) for h in range(2)]
+        banks = [psum.tile([P, PACK, H], F32, name=f"bank{h}") for h in range(2)]
+        for h in range(2):
+            interleave(nc.vector.tensor_copy, hid16[h][:], hid[h][:])
+        for h in range(2):
+            nc.vector.quantize_mx(
+                out=h_codes[h][:].bitcast(E5M2), scales=h_scales[h][:], in_=hid16[h][:].rearrange("p c t -> p (c t)")
+            )
+            for t in range(PACK):
                 nc.tensor.matmul_mx(
-                    out=bank[:, s, :],
-                    lhsT=wb_sb[:, t, :, :].rearrange("p q b -> p (q b)").bitcast(E2M1),
+                    out=banks[h][:, t, :],
+                    lhsT=wb_sb[:, t, :].bitcast(E2M1),
                     lhsT_scale=wbs_sb[:, t, :],
-                    rhs=h_codes[:].bitcast(E5M2),
-                    rhs_scale=h_scales[:],
+                    rhs=h_codes[h][:].bitcast(E5M2),
+                    rhs_scale=h_scales[h][:],
                     start=True,
                     stop=True,
                 )
-            rows = slice(2 * b, 2 * b + 2)
-            nc.vector.scalar_tensor_tensor(y[:, rows, :], rs_sb[:, rows, :], 0.5, bank[:], MULT, ADD)
-            nc.vector.scalar_tensor_tensor(
-                y[:, rows, 1:O], bank[:, :, 0 : O - 1], -0.7, y[:, rows, 1:O], MULT, ADD
-            )
-        nc.sync.dma_start(out=out_0.rearrange("(p t) o -> p t o", t=PACK), in_=y[:])
-        y16 = sb.tile([P, O, PACK], BF16, name="y16", align_bytes=64)
-        interleave(nc, y16[:], y[:])
+        y = [sb.tile([P, PACK, H], F32, name=f"y{h}") for h in range(2)]
+        y16 = [sb.tile([P, H, PACK], BF16, name=f"y16_{h}", align_bytes=64) for h in range(2)]
         y_codes = sb.tile([P, O], U32, name="y_codes", align_bytes=64)
         y_scales = sb.tile([P, O], U8, name="y_scales", align_bytes=64)
-        nc.vector.quantize_mx(
-            out=y_codes[:].bitcast(E4M3), scales=y_scales[:], in_=y16[:].rearrange("p c t -> p (c t)")
-        )
-        nc.sync.dma_start(out=out_1[0].rearrange("p c t -> p (c t)").bitcast(I32), in_=y_codes[:].bitcast(I32))
+        out_v = out_0.rearrange("(p t) o -> p t o", t=PACK)
+        words_v = out_1[0].rearrange("p c t -> p (c t)").bitcast(I32)
+        for h in range(2):
+            nc.vector.scalar_tensor_tensor(y[h][:], rs_sb[:, :, h * H : (h + 1) * H], 0.5, banks[h][:], MULT, ADD)
+        nc.vector.scalar_tensor_tensor(y[0][:, :, 1:H], banks[0][:, :, 0 : H - 1], -0.7, y[0][:, :, 1:H], MULT, ADD)
+        nc.vector.scalar_tensor_tensor(y[1][:, :, 0:1], banks[0][:, :, H - 1 : H], -0.7, y[1][:, :, 0:1], MULT, ADD)
+        nc.vector.scalar_tensor_tensor(y[1][:, :, 1:H], banks[1][:, :, 0 : H - 1], -0.7, y[1][:, :, 1:H], MULT, ADD)
+        for h in range(2):
+            cols = slice(h * H, (h + 1) * H)
+            nc.sync.dma_start(out=out_v[:, :, cols], in_=y[h][:])
+            interleave(nc.scalar.copy if h == 0 else nc.vector.tensor_copy, y16[h][:], y[h][:])
+            nc.vector.quantize_mx(
+                out=y_codes[:, cols].bitcast(E4M3), scales=y_scales[:, cols], in_=y16[h][:].rearrange("p c t -> p (c t)")
+            )
+            nc.sync.dma_start(out=words_v[:, cols], in_=y_codes[:, cols].bitcast(I32))
         for q in range(4):
-            eng = nc.scalar if q >= 1 else nc.sync
+            eng = nc.scalar if q >= 2 else nc.sync
             eng.dma_start(
                 out=out_2[0, 4 * q : 4 * q + 4, :].bitcast(I32),
                 in_=y_scales[32 * q : 32 * q + 4, :].bitcast(I32),

@@ -98,25 +98,25 @@ def tile_list_page_entryproducts_lagged_pl_kernel(
         nc.sync.dma_start(out=fk_sb[:], in_=fk.rearrange("(z p t) o -> p z (t o)", p=P, t=PACK))
         load_xb(0, 1)
         load_xa(0, 1)
-        load_ws(0)
-        load_ws(1)
         load_xa(0, 2)
-        load_ws(2)
-        load_ws(3)
+        for q in range(4):
+            load_ws(q)
         load_xb(1, 0)
         load_xa(0, 3)
         load_w(0)
         load_xa(1, 0)
-        nc.sync.dma_start(o3[:], offs3)
-        nc.sync.dma_start(o4[:], offs4)
         load_xb(1, 1)
         for t in range(1, PACK):
             load_xa(1, t)
         load_w(1)
         nc.sync.dma_start(out=wb_raw[:].bitcast(I32), in_=wb_words[0].bitcast(I32))
-        for t in range(PACK):
+        for q in range(4):
+            load_wbs(q)
+        nc.sync.dma_start(out=old_sb[0][:], in_=old_v[:, 0, :])
+        nc.sync.dma_start(o3[:], offs3)
+        nc.sync.dma_start(o4[:], offs4)
+        for t in range(1, PACK):
             nc.sync.dma_start(out=old_sb[t][:], in_=old_v[:, t, :])
-            load_wbs(t)
         nc.sync.dma_start(out=rs_sb[:], in_=rs.rearrange("(p t) o -> p t o", t=PACK))
 
         w_sb = [sb.tile([P, PACK, P], U32, name=f"w_sb{z}", align_bytes=64) for z in range(PASSES)]
@@ -156,8 +156,11 @@ def tile_list_page_entryproducts_lagged_pl_kernel(
                     stop=(z == PASSES - 1),
                 )
 
-        wb_sb = sb.tile([P, PACK, P], U16, name="wb_sb", tag="u16_1", align_bytes=64)
-        nc.vector.tensor_copy(out=wb_sb[:], in_=wb_raw[:].bitcast(U16).rearrange("p (q t) -> p t q", t=PACK))
+        wb_all = sb.tile([P, 3 * N], U8, name="wb_all", tag="u16_1", align_bytes=64)
+        wb_sb = wb_all[:, 0 : 2 * N].bitcast(U16).rearrange("p (t q) -> p t q", t=PACK)
+        wbs_sb = wb_all[:, 2 * N : 3 * N].rearrange("p (t q) -> p t q", t=PACK)
+        nc.vector.tensor_copy(out=wb_sb, in_=wb_raw[:].bitcast(U16).rearrange("p (q t) -> p t q", t=PACK))
+        nc.vector.tensor_copy(out=wbs_sb, in_=wbs_raw[:].rearrange("p (q t) -> p t q", t=PACK))
         ha = [sb.tile([P, J], F32, name=f"ha{t}") for t in range(PACK)]
         nc.scalar.activation(ha[0][:], acc[0][:], RELU)
         for t in range(1, PACK):
@@ -166,26 +169,26 @@ def tile_list_page_entryproducts_lagged_pl_kernel(
             nc.scalar.activation(placed[t][:].indirect(o3[:]), ha[t][:], COPY)
         nc.vector.tensor_copy(placed[1][:].indirect(o3[:]), ha[1][:])
         H = O // 2
-        hid = [sb.tile([P, PACK, H], BF16, name=f"hid{h}") for h in range(2)]
+        hid = [[sb.tile([P, 2, H], BF16, name=f"hid{h}{g}") for g in range(2)] for h in range(2)]
         for t in range(PACK):
             nc.vector.tensor_tensor(page[t][:], placed[t][:], old_sb[t][:], ADD)
             for h in range(2):
-                nc.scalar.activation(hid[h][:, t, :], page[t][:].indirect(o4[:, 8 * h : 8 * h + 8]), COPY)
-        wbs_sb = sb.tile([P, PACK, P], U8, name="wbs_sb", tag="old3", align_bytes=64)
-        nc.vector.tensor_copy(out=wbs_sb[:], in_=wbs_raw[:].rearrange("p (q t) -> p t q", t=PACK))
-        hid16 = [sb.tile([P, H, PACK], BF16, name=f"hid16_{h}", align_bytes=64) for h in range(2)]
+                nc.scalar.activation(hid[h][t // 2][:, t % 2, :], page[t][:].indirect(o4[:, 8 * h : 8 * h + 8]), COPY)
+        hid16 = sb.tile([P, 2, H, PACK], BF16, name="hid16", tag="old3", align_bytes=64)
         h_codes = [sb.tile([P, H], U32, name=f"h_codes{h}", align_bytes=64) for h in range(2)]
         h_scales = [sb.tile([P, H], U8, name=f"h_scales{h}", align_bytes=64) for h in range(2)]
-        banks = [psum.tile([P, PACK, H], F32, name=f"bank{h}") for h in range(2)]
-        for h in range(2):
-            interleave(nc.vector.tensor_copy, hid16[h][:], hid[h][:])
+        first = [psum.tile([P, 2, H], F32, name=f"first{g}") for g in range(2)]
+        second = psum.tile([P, PACK, H], F32, name="second")
+        for g in range(2):
+            for h in range(2):
+                interleave(nc.vector.tensor_copy, hid16[:, h, :, 2 * g : 2 * g + 2], hid[h][g][:])
         for h in range(2):
             nc.vector.quantize_mx(
-                out=h_codes[h][:].bitcast(E5M2), scales=h_scales[h][:], in_=hid16[h][:].rearrange("p c t -> p (c t)")
+                out=h_codes[h][:].bitcast(E5M2), scales=h_scales[h][:], in_=hid16[:, h, :, :].rearrange("p c t -> p (c t)")
             )
             for t in range(PACK):
                 nc.tensor.matmul_mx(
-                    out=banks[h][:, t, :],
+                    out=first[t // 2][:, t % 2, :] if h == 0 else second[:, t, :],
                     lhsT=wb_sb[:, t, :].bitcast(E2M1),
                     lhsT_scale=wbs_sb[:, t, :],
                     rhs=h_codes[h][:].bitcast(E5M2),
@@ -199,15 +202,24 @@ def tile_list_page_entryproducts_lagged_pl_kernel(
         y_scales = sb.tile([P, O], U8, name="y_scales", align_bytes=64)
         out_v = out_0.rearrange("(p t) o -> p t o", t=PACK)
         words_v = out_1[0].rearrange("p c t -> p (c t)").bitcast(I32)
-        for h in range(2):
-            nc.vector.scalar_tensor_tensor(y[h][:], rs_sb[:, :, h * H : (h + 1) * H], 0.5, banks[h][:], MULT, ADD)
-        nc.vector.scalar_tensor_tensor(y[0][:, :, 1:H], banks[0][:, :, 0 : H - 1], -0.7, y[0][:, :, 1:H], MULT, ADD)
-        nc.vector.scalar_tensor_tensor(y[1][:, :, 0:1], banks[0][:, :, H - 1 : H], -0.7, y[1][:, :, 0:1], MULT, ADD)
-        nc.vector.scalar_tensor_tensor(y[1][:, :, 1:H], banks[1][:, :, 0 : H - 1], -0.7, y[1][:, :, 1:H], MULT, ADD)
+        pairs = [slice(0, 2), slice(2, 4)]
+        for g in range(2):
+            nc.vector.scalar_tensor_tensor(y[0][:, pairs[g], :], rs_sb[:, pairs[g], 0:H], 0.5, first[g][:], MULT, ADD)
+        lag = nc.vector.scalar_tensor_tensor
+        lag(y[0][:, pairs[0], 1:H], first[0][:, :, 0 : H - 1], -0.7, y[0][:, pairs[0], 1:H], MULT, ADD)
+        nc.vector.scalar_tensor_tensor(y[1][:], rs_sb[:, :, H:O], 0.5, second[:], MULT, ADD)
+        lag(y[0][:, pairs[1], 1:H], first[1][:, :, 0 : H - 1], -0.7, y[0][:, pairs[1], 1:H], MULT, ADD)
+        lag(y[1][:, :, 1:H], second[:, :, 0 : H - 1], -0.7, y[1][:, :, 1:H], MULT, ADD)
+        for g in range(2):
+            lag(y[1][:, pairs[g], 0:1], first[g][:, :, H - 1 : H], -0.7, y[1][:, pairs[g], 0:1], MULT, ADD)
         for h in range(2):
             cols = slice(h * H, (h + 1) * H)
             nc.sync.dma_start(out=out_v[:, :, cols], in_=y[h][:])
-            interleave(nc.scalar.copy if h == 0 else nc.vector.tensor_copy, y16[h][:], y[h][:])
+            if h == 0:
+                interleave(nc.scalar.copy, y16[h][:], y[h][:])
+            else:
+                interleave(nc.vector.tensor_copy, y16[h][:, 0:88, :], y[h][:, :, 0:88])
+                interleave(nc.scalar.copy, y16[h][:, 88:H, :], y[h][:, :, 88:H])
             nc.vector.quantize_mx(
                 out=y_codes[:, cols].bitcast(E4M3), scales=y_scales[:, cols], in_=y16[h][:].rearrange("p c t -> p (c t)")
             )

@@ -62,7 +62,7 @@ def tile_list_page_entryproducts_lagged_pl_kernel(
         placed = [sb.tile([P, C], F32, name=f"placed{t}") for t in range(PACK)]
         page = [sb.tile([P, C], F32, name=f"page{t}") for t in range(PACK)]
 
-        nc.vector.memset(ws_raw[:].bitcast(I32), 0)
+        nc.gpsimd.memset(ws_raw[:].bitcast(I32), 0)
         nc.vector.memset(wbs_raw[:].bitcast(I32), 0)
         for t in range(PACK):
             nc.vector.memset(placed[t][:], 0.0)
@@ -91,29 +91,28 @@ def tile_list_page_entryproducts_lagged_pl_kernel(
         def load_xb(z, h):
             nc.sync.dma_start(out=xb_sb[z][h][:], in_=xb_v[z, :, 2 * h : 2 * h + 2, :])
 
+        load_w(0)
+        nc.sync.dma_start(o2[:], offs2)
+        for q in range(4):
+            load_ws(q)
         load_xb(0, 0)
         load_xa(0, 0)
-        nc.sync.dma_start(o2[:], offs2)
-        nc.sync.dma_start(o1[:], offs)
         nc.sync.dma_start(out=fk_sb[:], in_=fk.rearrange("(z p t) o -> p z (t o)", p=P, t=PACK))
         load_xb(0, 1)
+        nc.sync.dma_start(o1[:], offs)
         load_xa(0, 1)
         load_xa(0, 2)
         for q in range(4):
-            load_ws(q)
+            load_wbs(q)
         load_xb(1, 0)
         load_xa(0, 3)
-        load_w(0)
-        load_xa(1, 0)
         load_xb(1, 1)
-        for t in range(1, PACK):
+        for t in range(PACK):
             load_xa(1, t)
         load_w(1)
-        nc.sync.dma_start(out=wb_raw[:].bitcast(I32), in_=wb_words[0].bitcast(I32))
-        for q in range(4):
-            load_wbs(q)
-        nc.sync.dma_start(out=old_sb[0][:], in_=old_v[:, 0, :])
         nc.sync.dma_start(o3[:], offs3)
+        nc.sync.dma_start(out=wb_raw[:].bitcast(I32), in_=wb_words[0].bitcast(I32))
+        nc.sync.dma_start(out=old_sb[0][:], in_=old_v[:, 0, :])
         nc.sync.dma_start(o4[:], offs4)
         for t in range(1, PACK):
             nc.sync.dma_start(out=old_sb[t][:], in_=old_v[:, t, :])
@@ -122,6 +121,7 @@ def tile_list_page_entryproducts_lagged_pl_kernel(
         w_sb = [sb.tile([P, PACK, P], U32, name=f"w_sb{z}", align_bytes=64) for z in range(PASSES)]
         ws_sb = sb.tile([P, PASSES, PACK, P], U8, name="ws_sb", align_bytes=64)
 
+        wbs_sb = sb.tile([P, PACK, P], U8, name="wbs_sb", align_bytes=64)
         acc = [psum.tile([P, J], F32, name=f"acc{t}") for t in range(PACK)]
         for z in range(PASSES):
             u32 = [sb.tile([P, 2, J], F32, name=f"u32_{z}{h}") for h in range(2)]
@@ -135,11 +135,12 @@ def tile_list_page_entryproducts_lagged_pl_kernel(
                 if t % 2 == 1:
                     interleave(nc.vector.tensor_copy, u16[:, :, t - 1 : t + 1], u32[t // 2][:])
             nc.vector.tensor_copy(
-                out=w_sb[z][:].bitcast(I32),
-                in_=w_raw[z][:].bitcast(I32).rearrange("p (q t) -> p t q", t=PACK),
+                out=w_sb[z][:].bitcast(I32).rearrange("p t (c i) -> p c t i", i=4),
+                in_=w_raw[z][:].bitcast(I32).rearrange("p (c i t) -> p c t i", i=4, t=PACK),
             )
             if z == 0:
                 nc.vector.tensor_copy(out=ws_sb[:], in_=ws_raw[:].rearrange("p z (q t) -> p z t q", t=PACK))
+                nc.vector.tensor_copy(out=wbs_sb[:], in_=wbs_raw[:].rearrange("p (q t) -> p t q", t=PACK))
             u_codes = sb.tile([P, J], U32, name=f"u_codes{z}", align_bytes=64)
             u_scales = sb.tile([P, J], U8, name=f"u_scales{z}", align_bytes=64)
             nc.vector.quantize_mx(
@@ -156,11 +157,8 @@ def tile_list_page_entryproducts_lagged_pl_kernel(
                     stop=(z == PASSES - 1),
                 )
 
-        wb_all = sb.tile([P, 3 * N], U8, name="wb_all", tag="u16_1", align_bytes=64)
-        wb_sb = wb_all[:, 0 : 2 * N].bitcast(U16).rearrange("p (t q) -> p t q", t=PACK)
-        wbs_sb = wb_all[:, 2 * N : 3 * N].rearrange("p (t q) -> p t q", t=PACK)
-        nc.vector.tensor_copy(out=wb_sb, in_=wb_raw[:].bitcast(U16).rearrange("p (q t) -> p t q", t=PACK))
-        nc.vector.tensor_copy(out=wbs_sb, in_=wbs_raw[:].rearrange("p (q t) -> p t q", t=PACK))
+        wb_sb = sb.tile([P, PACK, P], U16, name="wb_sb", tag="u16_1", align_bytes=64)
+        nc.vector.tensor_copy(out=wb_sb[:], in_=wb_raw[:].bitcast(U16).rearrange("p (q t) -> p t q", t=PACK))
         ha = [sb.tile([P, J], F32, name=f"ha{t}") for t in range(PACK)]
         nc.scalar.activation(ha[0][:], acc[0][:], RELU)
         for t in range(1, PACK):

from contextlib import ExitStack

import concourse.mybir as mybir

K, T, J, S, R, C, O, N = 1024, 1024, 256, 512, 512, 1024, 256, 512
FLOPS = 2 * K * R * J + 2 * R * N * O

F32 = mybir.dt.float32
BF16 = mybir.dt.bfloat16
I32 = mybir.dt.int32
U32 = mybir.dt.uint32
U16 = mybir.dt.uint16
U8 = mybir.dt.uint8
E5M2 = mybir.dt.float8_e5m2_x4
E4M3 = mybir.dt.float8_e4m3fn_x4
E2M1 = mybir.dt.float4_e2m1fn_x4
MULT = mybir.AluOpType.mult
ADD = mybir.AluOpType.add
COPY = mybir.ActivationFunctionType.Copy
RELU = mybir.ActivationFunctionType.Relu

P = 128
PACK = 4
PASSES = K // (P * PACK)


def interleave(copy, dst, src):
    copy(
        out=dst.rearrange("p (c i) t -> p c t i", i=4),
        in_=src.rearrange("p t (c i) -> p c t i", i=4),
    )


def tile_list_page_entryproducts_lagged_pl_kernel(
    tc, xa, xb, fk, w_words, w_scales, oldh, wb_words, wb_scales, rs,
    offs, offs2, offs3, offs4, out_0, out_1, out_2,
):
    nc = tc.nc
    with ExitStack() as ctx:
        lists = ctx.enter_context(tc.tile_pool(name="lists", bufs=1))
        sb = ctx.enter_context(tc.tile_pool(name="sb", bufs=1))
        psum = ctx.enter_context(tc.psum_pool(name="psum", bufs=1))

        o1 = lists.tile([P, J // 16], U16, name="o1")
        o2 = lists.tile([P, J // 16], U16, name="o2")
        o3 = lists.tile([P, J // 16], U16, name="o3")
        o4 = lists.tile([P, O // 16], U16, name="o4")

        xa_v = xa.rearrange("(z p t) c -> z p t c", p=P, t=PACK)
        xb_v = xb.rearrange("(z p t) c -> z p t c", p=P, t=PACK)
        old_v = oldh.rearrange("(p t) c -> p t c", t=PACK)

        xa_sb = [[sb.tile([P, T], F32, name=f"xa{z}{t}") for t in range(PACK)] for z in range(PASSES)]
        xb_sb = [[sb.tile([P, 2, S], F32, name=f"xb{z}{h}") for h in range(2)] for z in range(PASSES)]
        fk_sb = sb.tile([P, PASSES, PACK], F32, name="fk_sb")
        w_raw = [sb.tile([P, R], U32, name=f"w_raw{z}") for z in range(PASSES)]
        ws_raw = sb.tile([P, PASSES, R], U8, name="ws_raw")
        wb_raw = sb.tile([P, 2 * N], U8, name="wb_raw")
        wbs_raw = sb.tile([P, N], U8, name="wbs_raw")
        old_sb = [sb.tile([P, C], F32, name=f"old{t}", tag=f"old{t}", align_bytes=64) for t in range(PACK)]
        rs_sb = sb.tile([P, PACK, O], F32, name="rs_sb")
        placed = [sb.tile([P, C], F32, name=f"placed{t}") for t in range(PACK)]
        page = [sb.tile([P, C], F32, name=f"page{t}") for t in range(PACK)]

        nc.gpsimd.memset(ws_raw[:].bitcast(I32), 0)
        nc.vector.memset(wbs_raw[:].bitcast(I32), 0)
        for t in range(PACK):
            nc.vector.memset(placed[t][:], 0.0)

        def load_w(z):
            nc.sync.dma_start(
                out=w_raw[z][:].bitcast(I32),
                in_=w_words[z].rearrange("p c t -> p (c t)").bitcast(I32),
            )

        def load_xa(z, t):
            nc.sync.dma_start(out=xa_sb[z][t][:], in_=xa_v[z, :, t, :])

        def load_ws(q):
            nc.sync.dma_start(
                out=ws_raw[32 * q : 32 * q + 4, :, :].bitcast(I32),
                in_=w_scales[:, 4 * q : 4 * q + 4, :].rearrange("z r c -> r z c").bitcast(I32),
            )

        def load_wbs(q):
            nc.sync.dma_start(
                out=wbs_raw[32 * q : 32 * q + 4, :].bitcast(I32),
                in_=wb_scales[0, 4 * q : 4 * q + 4, :].bitcast(I32),
            )

        def load_xb(z, h):
            nc.sync.dma_start(out=xb_sb[z][h][:], in_=xb_v[z, :, 2 * h : 2 * h + 2, :])

        load_w(0)
        nc.sync.dma_start(o2[:], offs2)
        for q in range(4):
            load_ws(q)
        load_xb(0, 0)
        load_xa(0, 0)
        nc.sync.dma_start(out=fk_sb[:], in_=fk.rearrange("(z p t) o -> p z (t o)", p=P, t=PACK))
        load_xb(0, 1)
        nc.sync.dma_start(o1[:], offs)
        load_xa(0, 1)
        load_xa(0, 2)
        for q in range(4):
            load_wbs(q)
        load_xb(1, 0)
        load_xa(0, 3)
        load_xb(1, 1)
        for t in range(PACK):
            load_xa(1, t)
        load_w(1)
        nc.sync.dma_start(o3[:], offs3)
        nc.sync.dma_start(out=wb_raw[:].bitcast(I32), in_=wb_words[0].bitcast(I32))
        nc.sync.dma_start(out=old_sb[0][:], in_=old_v[:, 0, :])
        nc.sync.dma_start(o4[:], offs4)
        for t in range(1, PACK):
            nc.sync.dma_start(out=old_sb[t][:], in_=old_v[:, t, :])
        nc.sync.dma_start(out=rs_sb[:], in_=rs.rearrange("(p t) o -> p t o", t=PACK))

        w_sb = [sb.tile([P, PACK, P], U32, name=f"w_sb{z}", align_bytes=64) for z in range(PASSES)]
        ws_sb = sb.tile([P, PASSES, PACK, P], U8, name="ws_sb", align_bytes=64)

        wbs_sb = sb.tile([P, PACK, P], U8, name="wbs_sb", align_bytes=64)
        acc = [psum.tile([P, J], F32, name=f"acc{t}") for t in range(PACK)]
        for z in range(PASSES):
            u32 = [sb.tile([P, 2, J], F32, name=f"u32_{z}{h}") for h in range(2)]
            u16 = sb.tile([P, J, PACK], BF16, name=f"u16_{z}", tag=f"u16_{z}", align_bytes=64)
            for t in range(PACK):
                picked = sb.tile([P, J], F32, name=f"picked{z}{t}")
                scaled = sb.tile([P, J], F32, name=f"scaled{z}{t}")
                nc.scalar.activation(picked[:], xb_sb[z][t // 2][:, t % 2, :].indirect(o2[:]), COPY)
                nc.scalar.activation(scaled[:], picked[:], COPY, scale=fk_sb[:, z, t : t + 1])
                nc.vector.tensor_tensor(u32[t // 2][:, t % 2, :], xa_sb[z][t][:].indirect(o1[:]), scaled[:], MULT)
                if t % 2 == 1:
                    interleave(nc.vector.tensor_copy, u16[:, :, t - 1 : t + 1], u32[t // 2][:])
            nc.vector.tensor_copy(
                out=w_sb[z][:].bitcast(I32).rearrange("p t (c i) -> p c t i", i=4),
                in_=w_raw[z][:].bitcast(I32).rearrange("p (c i t) -> p c t i", i=4, t=PACK),
            )
            if z == 0:
                nc.vector.tensor_copy(out=ws_sb[:], in_=ws_raw[:].rearrange("p z (q t) -> p z t q", t=PACK))
                nc.vector.tensor_copy(out=wbs_sb[:], in_=wbs_raw[:].rearrange("p (q t) -> p t q", t=PACK))
            u_codes = sb.tile([P, J], U32, name=f"u_codes{z}", align_bytes=64)
            u_scales = sb.tile([P, J], U8, name=f"u_scales{z}", align_bytes=64)
            nc.vector.quantize_mx(
                out=u_codes[:].bitcast(E5M2), scales=u_scales[:], in_=u16[:].rearrange("p c t -> p (c t)")
            )
            for t in range(PACK):
                nc.tensor.matmul_mx(
                    out=acc[t][:],
                    lhsT=w_sb[z][:, t, :].bitcast(E5M2),
                    lhsT_scale=ws_sb[:, z, t, :],
                    rhs=u_codes[:].bitcast(E5M2),
                    rhs_scale=u_scales[:],
                    start=(z == 0),
                    stop=(z == PASSES - 1),
                )

        wb_sb = sb.tile([P, PACK, P], U16, name="wb_sb", tag="u16_1", align_bytes=64)
        nc.vector.tensor_copy(out=wb_sb[:], in_=wb_raw[:].bitcast(U16).rearrange("p (q t) -> p t q", t=PACK))
        ha = [sb.tile([P, J], F32, name=f"ha{t}") for t in range(PACK)]
        nc.scalar.activation(ha[0][:], acc[0][:], RELU)
        for t in range(1, PACK):
            nc.vector.tensor_scalar_max(ha[t][:], acc[t][:], 0.0)
        for t in (0, 2, 3):
            nc.scalar.activation(placed[t][:].indirect(o3[:]), ha[t][:], COPY)
        nc.vector.tensor_copy(placed[1][:].indirect(o3[:]), ha[1][:])
        H = O // 2
        hid = [[sb.tile([P, 2, H], BF16, name=f"hid{h}{g}") for g in range(2)] for h in range(2)]
        for t in range(PACK):
            nc.vector.tensor_tensor(page[t][:], placed[t][:], old_sb[t][:], ADD)
            for h in range(2):
                nc.scalar.activation(hid[h][t // 2][:, t % 2, :], page[t][:].indirect(o4[:, 8 * h : 8 * h + 8]), COPY)
        hid16 = sb.tile([P, 2, H, PACK], BF16, name="hid16", tag="old3", align_bytes=64)
        h_codes = [sb.tile([P, H], U32, name=f"h_codes{h}", align_bytes=64) for h in range(2)]
        h_scales = [sb.tile([P, H], U8, name=f"h_scales{h}", align_bytes=64) for h in range(2)]
        first = [psum.tile([P, 2, H], F32, name=f"first{g}") for g in range(2)]
        second = psum.tile([P, PACK, H], F32, name="second")
        for g in range(2):
            for h in range(2):
                interleave(nc.vector.tensor_copy, hid16[:, h, :, 2 * g : 2 * g + 2], hid[h][g][:])
        for h in range(2):
            nc.vector.quantize_mx(
                out=h_codes[h][:].bitcast(E5M2), scales=h_scales[h][:], in_=hid16[:, h, :, :].rearrange("p c t -> p (c t)")
            )
            for t in range(PACK):
                nc.tensor.matmul_mx(
                    out=first[t // 2][:, t % 2, :] if h == 0 else second[:, t, :],
                    lhsT=wb_sb[:, t, :].bitcast(E2M1),
                    lhsT_scale=wbs_sb[:, t, :],
                    rhs=h_codes[h][:].bitcast(E5M2),
                    rhs_scale=h_scales[h][:],
                    start=True,
                    stop=True,
                )
        y = [sb.tile([P, PACK, H], F32, name=f"y{h}") for h in range(2)]
        y16 = [sb.tile([P, H, PACK], BF16, name=f"y16_{h}", align_bytes=64) for h in range(2)]
        y_codes = sb.tile([P, O], U32, name="y_codes", align_bytes=64)
        y_scales = sb.tile([P, O], U8, name="y_scales", align_bytes=64)
        out_v = out_0.rearrange("(p t) o -> p t o", t=PACK)
        words_v = out_1[0].rearrange("p c t -> p (c t)").bitcast(I32)
        pairs = [slice(0, 2), slice(2, 4)]
        for g in range(2):
            nc.vector.scalar_tensor_tensor(y[0][:, pairs[g], :], rs_sb[:, pairs[g], 0:H], 0.5, first[g][:], MULT, ADD)
        lag = nc.vector.scalar_tensor_tensor
        lag(y[0][:, pairs[0], 1:H], first[0][:, :, 0 : H - 1], -0.7, y[0][:, pairs[0], 1:H], MULT, ADD)
        nc.vector.scalar_tensor_tensor(y[1][:], rs_sb[:, :, H:O], 0.5, second[:], MULT, ADD)
        lag(y[0][:, pairs[1], 1:H], first[1][:, :, 0 : H - 1], -0.7, y[0][:, pairs[1], 1:H], MULT, ADD)
        lag(y[1][:, :, 1:H], second[:, :, 0 : H - 1], -0.7, y[1][:, :, 1:H], MULT, ADD)
        for g in range(2):
            lag(y[1][:, pairs[g], 0:1], first[g][:, :, H - 1 : H], -0.7, y[1][:, pairs[g], 0:1], MULT, ADD)
        for h in range(2):
            cols = slice(h * H, (h + 1) * H)
            nc.sync.dma_start(out=out_v[:, :, cols], in_=y[h][:])
            if h == 0:
                interleave(nc.scalar.copy, y16[h][:], y[h][:])
            else:
                interleave(nc.vector.tensor_copy, y16[h][:, 0:88, :], y[h][:, :, 0:88])
                interleave(nc.scalar.copy, y16[h][:, 88:H, :], y[h][:, :, 88:H])
            nc.vector.quantize_mx(
                out=y_codes[:, cols].bitcast(E4M3), scales=y_scales[:, cols], in_=y16[h][:].rearrange("p c t -> p (c t)")
            )
            nc.sync.dma_start(out=words_v[:, cols], in_=y_codes[:, cols].bitcast(I32))
        for q in range(4):
            eng = nc.scalar if q >= 2 else nc.sync
            eng.dma_start(
                out=out_2[0, 4 * q : 4 * q + 4, :].bitcast(I32),
                in_=y_scales[32 * q : 32 * q + 4, :].bitcast(I32),
            )
